import numpy as np
CORES = [1,0]
N = 2
PERM = [[0,1],[1,0]]
def setup_inputs(rng):
    return {"x": rng.standard_normal((N, 128, 16384), dtype=np.float32)}
def reference(x):
    y = np.empty_like(x)
    for s, d in PERM:
        y[d] = x[s]
    return {"y": y}

SCRATCH = {
    "stage": ("sbuf", [128, 16384], "float32"),
    "land": ("sbuf", [128, 16384], "float32"),
}
SEMAPHORES = ["loaded", "read", "arrived", "stored"]

ENGINES = 16


def rank_program(g, core, T, topo):
    rank = T.rank_of(core)
    if rank is None:
        return

    perm = T.tables["PERM"]
    dsts = [d for s, d in perm if s == rank]
    srcs = [s for s, d in perm if d == rank]
    remote_dsts = [d for d in dsts if d != rank]
    sem = T.sem

    if remote_dsts:
        g.dma_start(T.stage[:], T.x[:]).then_inc(sem.loaded, ENGINES)
        g.wait_ge(sem.loaded, ENGINES)
        for d in remote_dsts:
            dst_core = T.cores[d]
            rid, pid = topo.addr(dst_core)[:2]
            g.remote_dma(T.land[:], T.stage[:], sem.arrived, sem.read, pid, rid, topo.mask(core, dst_core))

    if srcs:
        if srcs[0] == rank:
            g.dma_start(T.y[:], T.x[:]).then_inc(sem.stored, ENGINES)
        else:
            g.wait_ge(sem.arrived, ENGINES)
            g.dma_start(T.y[:], T.land[:]).then_inc(sem.stored, ENGINES)
        g.wait_ge(sem.stored, ENGINES)

    if remote_dsts:
        g.wait_ge(sem.read, ENGINES * len(remote_dsts))
